import numpy as np
import ml_dtypes


def mxq(x, axis, fmt="e4m3"):
    dtype, down = {"e4m3": (ml_dtypes.float8_e4m3fn, 7), "e5m2": (ml_dtypes.float8_e5m2, 14)}[fmt]
    v = np.moveaxis(np.asarray(x, np.float32).astype(ml_dtypes.bfloat16).astype(np.float64), axis, -1)
    blocks = v.reshape(v.shape[:-1] + (-1, 32))
    amax = np.abs(blocks).max(-1, keepdims=True)
    byte = np.maximum(np.where(amax > 0, np.frexp(amax)[1] - 1 + 127, 0) - down, 1)
    scale = np.exp2(byte - 127.0)
    codes = (blocks / scale).astype(np.float32).astype(dtype).astype(np.float64)
    return np.moveaxis((codes * scale).reshape(v.shape), -1, axis)


WIDE = False


def mx_kscale(k):
    if not WIDE:
        return np.ones(k)
    levels = np.array([10, -10, 5, -5, 0])
    if k % 512:
        return np.exp2(np.random.permutation(np.resize(levels, k // 32))).repeat(32)
    a = np.empty((k // 512, 16))
    for p in range(k // 512):
        a[p, :8] = np.random.permutation(np.resize(levels, 8))
        for g in range(8):
            far = levels[np.abs(levels - a[p, g]) >= 10]
            a[p, g + 8] = far[np.random.randint(len(far))]
    return np.exp2(a.ravel()).repeat(32)


def f64(x):
    return np.asarray(x).astype(np.float64)


def striped(idx):
    return np.tile(idx.reshape(-1, 16).T, (8, 1)).astype(np.uint16)


def unstriped(offs):
    return offs[:16].T.reshape(-1).astype(np.int64)


def pack_weight(w):
    k, n = w.shape
    w = f64(np.asarray(w, np.float32).astype(ml_dtypes.bfloat16)).reshape(k // 32, 32, n)
    amax = np.abs(w).max(1)
    byte = np.clip(np.where(amax > 0, np.frexp(amax)[1] - 1 + 127 - 7, 1), 1, 254)
    scaled = (w * np.exp2(127.0 - byte)[:, None, :]).reshape(k, n).astype(np.float32)
    words = np.ascontiguousarray(scaled.reshape(k // 512, 128, 4, n).transpose(0, 1, 3, 2)).astype(ml_dtypes.float8_e4m3fn).view(np.uint8)
    return words, np.ascontiguousarray(byte.astype(np.uint8).reshape(k // 512, 16, n))


def unpack_weight(words, scales):
    g, p, n, _ = words.shape
    vals = np.ascontiguousarray(words).view(ml_dtypes.float8_e4m3fn).astype(np.float64) * np.repeat(np.exp2(scales.astype(np.float64) - 127.0), 8, axis=1)[..., None]
    return vals.transpose(0, 1, 3, 2).reshape(g * 512, n)


K, T, N, U = 1024, 512, 128, 1024


def setup_inputs():
    n = np.random.standard_normal
    s = mx_kscale(K)[:, None]
    packed_xT = pack_weight(n((K, T)) * s)
    return {
        "x_words": packed_xT[0],
        "x_scales": packed_xT[1],
        "mem": n((N, U)).astype(np.float32),
        "w1": (n((K, N)) / np.sqrt(K) / s).astype(np.float32),
        "slot": striped(np.random.permutation(U)[:T]),
    }


def reference(x_words, x_scales, mem, w1, slot):
    xq = unpack_weight(x_words, x_scales)
    y = mxq(f64(w1), 0, "e4m3").T @ xq
    out = f64(mem).copy()
    out[:, unstriped(slot)] = np.minimum(f64(mem)[:, unstriped(slot)], y)
    return out

@@ -1,0 +1,85 @@
+from contextlib import ExitStack
+
+import concourse.mybir as mybir
+
+K, T, N, U = 1024, 512, 128, 1024
+FLOPS = 2 * K * T * N
+
+F32 = mybir.dt.float32
+BF16 = mybir.dt.bfloat16
+I32 = mybir.dt.int32
+U32 = mybir.dt.uint32
+U16 = mybir.dt.uint16
+U8 = mybir.dt.uint8
+FP8X4 = mybir.dt.float8_e4m3fn_x4
+MIN = mybir.AluOpType.min
+
+P = 128
+PACK = 4
+PASSES = K // (P * PACK)
+X_LOADS = ((0, 128), (128, 256), (256, 512))
+PIECES = ((0, 128), (128, 256), (256, 512))
+SCATTER_AFTER = {128: ((0, 128),), 256: ((128, 512),)}
+GATHERS = ((0, 256), (256, 512))
+
+
+def tile_picked_widxput_min_l_kernel(tc, x_words, x_scales, mem, w1, slot, out):
+    nc = tc.nc
+    with ExitStack() as ctx:
+        keep = ctx.enter_context(tc.tile_pool(name="keep", bufs=1))
+        psum = ctx.enter_context(tc.psum_pool(name="psum", bufs=1))
+
+        offsets = keep.tile([P, T // 16], U16, name="offsets")
+        store = keep.tile([P, U], F32, name="store")
+        x_plane = keep.tile([P, PASSES, T], U8, name="x_plane", align_bytes=64)
+        w_raw = [keep.tile([P, PACK, N], F32, name="w_raw%d" % g) for g in range(PASSES)]
+        x_codes = [keep.tile([P, PASSES, b - a], U32, name="x_codes%d" % a, align_bytes=64) for a, b in X_LOADS]
+
+        for g in range(PASSES):
+            nc.sync.dma_start(out=w_raw[g][:], in_=w1[g * P * PACK : (g + 1) * P * PACK, :].rearrange("(p j) m -> p j m", j=PACK))
+            if g == 0:
+                nc.sync.dma_start(offsets[:], slot)
+        nc.sync.dma_start(out=store[:], in_=mem)
+        words = x_words.rearrange("z p c r -> p z (c r)")
+        for (a, b), t in zip(X_LOADS, x_codes):
+            nc.sync.dma_start(out=t[:].bitcast(I32), in_=words[:, :, PACK * a : PACK * b].bitcast(I32))
+        rows = x_scales.rearrange("z (q r) c -> r q z c", r=4)
+        for r in range(4):
+            nc.scalar.dma_start(out=x_plane[r:P:32, :, :].bitcast(I32), in_=rows[r].bitcast(I32))
+
+        w_codes, w_plane = [], []
+        grouped = []
+        for g in range(PASSES):
+            t = keep.tile([P, N, PACK], BF16, name="grouped%d" % g, align_bytes=64)
+            nc.vector.tensor_copy(out=t[:].rearrange("p (c i) j -> p c j i", i=4), in_=w_raw[g][:].rearrange("p j (c i) -> p c j i", i=4))
+            grouped.append(t)
+        for g in range(PASSES):
+            c = keep.tile([P, N], U32, name="w_codes%d" % g, align_bytes=64)
+            s = keep.tile([P, N], U8, name="w_plane%d" % g, align_bytes=64)
+            nc.vector.quantize_mx(out=c[:].bitcast(FP8X4), scales=s[:], in_=grouped[g][:].rearrange("p m j -> p (m j)"))
+            w_codes.append(c)
+            w_plane.append(s)
+
+        old = keep.tile([P, T], F32, name="old")
+        for a, b in GATHERS:
+            nc.vector.tensor_copy(old[:, a:b], store[:].indirect(offsets[:, a // 16 : b // 16]))
+
+        new = keep.tile([P, T], F32, name="new")
+        for a, b in PIECES:
+            y = psum.tile([P, b - a], F32, name="y%d" % a)
+            h = [i for i, (xa, xb) in enumerate(X_LOADS) if xa <= a < xb][0]
+            xa = X_LOADS[h][0]
+            for g in range(PASSES):
+                nc.tensor.matmul_mx(
+                    out=y[:],
+                    lhsT=w_codes[g][:].bitcast(FP8X4),
+                    lhsT_scale=w_plane[g][:],
+                    rhs=x_codes[h][:, g, a - xa : b - xa].bitcast(FP8X4),
+                    rhs_scale=x_plane[:, g, a:b],
+                    start=(g == 0),
+                    stop=(g == PASSES - 1),
+                )
+            nc.vector.tensor_tensor(new[:, a:b], y[:], old[:, a:b], MIN)
+            for sa, sb in SCATTER_AFTER.get(a, ()):
+                nc.vector.tensor_copy(store[:].indirect(offsets[:, sa // 16 : sb // 16]), new[:, sa:sb])
+        nc.sync.dma_start(out=out, in_=store[:])

@@ -17,9 +17,9 @@ MIN = mybir.AluOpType.min
 P = 128
 PACK = 4
 PASSES = K // (P * PACK)
-X_LOADS = ((0, 128), (128, 256), (256, 512))
-PIECES = ((0, 128), (128, 256), (256, 512))
-SCATTER_AFTER = {128: ((0, 128),), 256: ((128, 512),)}
+HALVES = ((0, 256), (256, 512))
+MINIMA = {0: ((0, 128), (128, 256)), 256: ((256, 512),)}
+SCATTER_AFTER = {0: (0, 128), 256: (128, 512)}
 GATHERS = ((0, 256), (256, 512))
 
 
@@ -33,7 +33,7 @@ def tile_picked_widxput_min_l_kernel(tc, x_words, x_scales, mem, w1, slot, out):
         store = keep.tile([P, U], F32, name="store")
         x_plane = keep.tile([P, PASSES, T], U8, name="x_plane", align_bytes=64)
         w_raw = [keep.tile([P, PACK, N], F32, name="w_raw%d" % g) for g in range(PASSES)]
-        x_codes = [keep.tile([P, PASSES, b - a], U32, name="x_codes%d" % a, align_bytes=64) for a, b in X_LOADS]
+        x_codes = [keep.tile([P, PASSES, b - a], U32, name="x_codes%d" % a, align_bytes=64) for a, b in HALVES]
 
         for g in range(PASSES):
             nc.sync.dma_start(out=w_raw[g][:], in_=w1[g * P * PACK : (g + 1) * P * PACK, :].rearrange("(p j) m -> p j m", j=PACK))
@@ -41,7 +41,7 @@ def tile_picked_widxput_min_l_kernel(tc, x_words, x_scales, mem, w1, slot, out):
                 nc.sync.dma_start(offsets[:], slot)
         nc.sync.dma_start(out=store[:], in_=mem)
         words = x_words.rearrange("z p c r -> p z (c r)")
-        for (a, b), t in zip(X_LOADS, x_codes):
+        for (a, b), t in zip(HALVES, x_codes):
             nc.sync.dma_start(out=t[:].bitcast(I32), in_=words[:, :, PACK * a : PACK * b].bitcast(I32))
         rows = x_scales.rearrange("z (q r) c -> r q z c", r=4)
         for r in range(4):
@@ -65,21 +65,20 @@ def tile_picked_widxput_min_l_kernel(tc, x_words, x_scales, mem, w1, slot, out):
             nc.vector.tensor_copy(old[:, a:b], store[:].indirect(offsets[:, a // 16 : b // 16]))
 
         new = keep.tile([P, T], F32, name="new")
-        for a, b in PIECES:
+        for h, (a, b) in enumerate(HALVES):
             y = psum.tile([P, b - a], F32, name="y%d" % a)
-            h = [i for i, (xa, xb) in enumerate(X_LOADS) if xa <= a < xb][0]
-            xa = X_LOADS[h][0]
             for g in range(PASSES):
                 nc.tensor.matmul_mx(
                     out=y[:],
                     lhsT=w_codes[g][:].bitcast(FP8X4),
                     lhsT_scale=w_plane[g][:],
-                    rhs=x_codes[h][:, g, a - xa : b - xa].bitcast(FP8X4),
+                    rhs=x_codes[h][:, g, :].bitcast(FP8X4),
                     rhs_scale=x_plane[:, g, a:b],
                     start=(g == 0),
                     stop=(g == PASSES - 1),
                 )
-            nc.vector.tensor_tensor(new[:, a:b], y[:], old[:, a:b], MIN)
-            for sa, sb in SCATTER_AFTER.get(a, ()):
-                nc.vector.tensor_copy(store[:].indirect(offsets[:, sa // 16 : sb // 16]), new[:, sa:sb])
+            for ma, mb in MINIMA[a]:
+                nc.vector.tensor_tensor(new[:, ma:mb], y[:, ma - a : mb - a], old[:, ma:mb], MIN)
+            sa, sb = SCATTER_AFTER[a]
+            nc.vector.tensor_copy(store[:].indirect(offsets[:, sa // 16 : sb // 16]), new[:, sa:sb])
         nc.sync.dma_start(out=out, in_=store[:])

@@ -33,7 +33,9 @@ def tile_picked_widxput_min_l_kernel(tc, x_words, x_scales, mem, w1, slot, out):
         store = keep.tile([P, U], F32, name="store")
         x_plane = keep.tile([P, PASSES, T], U8, name="x_plane", align_bytes=64)
         w_raw = [keep.tile([P, PACK, N], F32, name="w_raw%d" % g) for g in range(PASSES)]
-        x_codes = [keep.tile([P, PASSES, b - a], U32, name="x_codes%d" % a, align_bytes=64) for a, b in HALVES]
+        x_first = [keep.tile([P, HALVES[0][1]], U32, name="x_first%d" % g, align_bytes=64) for g in range(PASSES)]
+        x_second = keep.tile([P, PASSES, T - HALVES[0][1]], U32, name="x_second", align_bytes=64)
+        x_codes = [[x_first[g][:] for g in range(PASSES)], [x_second[:, g, :] for g in range(PASSES)]]
 
         for g in range(PASSES):
             nc.sync.dma_start(out=w_raw[g][:], in_=w1[g * P * PACK : (g + 1) * P * PACK, :].rearrange("(p j) m -> p j m", j=PACK))
@@ -41,8 +43,10 @@ def tile_picked_widxput_min_l_kernel(tc, x_words, x_scales, mem, w1, slot, out):
                 nc.sync.dma_start(offsets[:], slot)
         nc.sync.dma_start(out=store[:], in_=mem)
         words = x_words.rearrange("z p c r -> p z (c r)")
-        for (a, b), t in zip(HALVES, x_codes):
-            nc.sync.dma_start(out=t[:].bitcast(I32), in_=words[:, :, PACK * a : PACK * b].bitcast(I32))
+        cut = PACK * HALVES[0][1]
+        for g in range(PASSES):
+            nc.sync.dma_start(out=x_first[g][:].bitcast(I32), in_=words[:, g, :cut].bitcast(I32))
+        nc.sync.dma_start(out=x_second[:].bitcast(I32), in_=words[:, :, cut:].bitcast(I32))
         rows = x_scales.rearrange("z (q r) c -> r q z c", r=4)
         for r in range(4):
             nc.scalar.dma_start(out=x_plane[r:P:32, :, :].bitcast(I32), in_=rows[r].bitcast(I32))
@@ -66,19 +70,20 @@ def tile_picked_widxput_min_l_kernel(tc, x_words, x_scales, mem, w1, slot, out):
 
         new = keep.tile([P, T], F32, name="new")
         for h, (a, b) in enumerate(HALVES):
-            y = psum.tile([P, b - a], F32, name="y%d" % a)
+            y = {ma: psum.tile([P, mb - ma], F32, name="y%d" % ma) for ma, mb in MINIMA[a]}
             for g in range(PASSES):
-                nc.tensor.matmul_mx(
-                    out=y[:],
-                    lhsT=w_codes[g][:].bitcast(FP8X4),
-                    lhsT_scale=w_plane[g][:],
-                    rhs=x_codes[h][:, g, :].bitcast(FP8X4),
-                    rhs_scale=x_plane[:, g, a:b],
-                    start=(g == 0),
-                    stop=(g == PASSES - 1),
-                )
+                for ma, mb in MINIMA[a]:
+                    nc.tensor.matmul_mx(
+                        out=y[ma][:],
+                        lhsT=w_codes[g][:].bitcast(FP8X4),
+                        lhsT_scale=w_plane[g][:],
+                        rhs=x_codes[h][g][:, ma - a : mb - a].bitcast(FP8X4),
+                        rhs_scale=x_plane[:, g, ma:mb],
+                        start=(g == 0),
+                        stop=(g == PASSES - 1),
+                    )
             for ma, mb in MINIMA[a]:
-                nc.vector.tensor_tensor(new[:, ma:mb], y[:, ma - a : mb - a], old[:, ma:mb], MIN)
+                nc.vector.tensor_tensor(new[:, ma:mb], y[ma][:], old[:, ma:mb], MIN)
             sa, sb = SCATTER_AFTER[a]
             nc.vector.tensor_copy(store[:].indirect(offsets[:, sa // 16 : sb // 16]), new[:, sa:sb])
         nc.sync.dma_start(out=out, in_=store[:])

@@ -68,6 +68,8 @@ def tile_picked_widxput_min_l_kernel(tc, x_words, x_scales, mem, w1, slot, out):
         for a, b in GATHERS:
             nc.vector.tensor_copy(old[:, a:b], store[:].indirect(offsets[:, a // 16 : b // 16]))
 
+        nc.scalar.dma_start(out=out[:, 0:8], in_=old[:, 0:8])
+
         new = keep.tile([P, T], F32, name="new")
         for h, (a, b) in enumerate(HALVES):
             y = {ma: psum.tile([P, mb - ma], F32, name="y%d" % ma) for ma, mb in MINIMA[a]}

@@ -39,8 +39,7 @@ def tile_picked_widxput_min_l_kernel(tc, x_words, x_scales, mem, w1, slot, out):
 
         for g in range(PASSES):
             nc.sync.dma_start(out=w_raw[g][:], in_=w1[g * P * PACK : (g + 1) * P * PACK, :].rearrange("(p j) m -> p j m", j=PACK))
-            if g == 0:
-                nc.sync.dma_start(offsets[:], slot)
+        nc.sync.dma_start(offsets[:], slot)
         nc.sync.dma_start(out=store[:], in_=mem)
         words = x_words.rearrange("z p c r -> p z (c r)")
         cut = PACK * HALVES[0][1]
@@ -67,8 +66,6 @@ def tile_picked_widxput_min_l_kernel(tc, x_words, x_scales, mem, w1, slot, out):
         old = keep.tile([P, T], F32, name="old")
         for a, b in GATHERS:
             nc.vector.tensor_copy(old[:, a:b], store[:].indirect(offsets[:, a // 16 : b // 16]))
-
-        nc.scalar.dma_start(out=out[:, 0:8], in_=old[:, 0:8])
 
         new = keep.tile([P, T], F32, name="new")
         for h, (a, b) in enumerate(HALVES):

@@ -37,8 +37,18 @@ def tile_picked_widxput_min_l_kernel(tc, x_words, x_scales, mem, w1, slot, out):
         x_second = keep.tile([P, PASSES, T - HALVES[0][1]], U32, name="x_second", align_bytes=64)
         x_codes = [[x_first[g][:] for g in range(PASSES)], [x_second[:, g, :] for g in range(PASSES)]]
 
+        rows = x_scales.rearrange("z (q r) c -> r q z c", r=4)
+
+        def load_scales(queue, r):
+            queue.dma_start(out=x_plane[r:P:32, :, :].bitcast(I32), in_=rows[r].bitcast(I32))
+
+        for r in (0, 1):
+            load_scales(nc.scalar, r)
         for g in range(PASSES):
             nc.sync.dma_start(out=w_raw[g][:], in_=w1[g * P * PACK : (g + 1) * P * PACK, :].rearrange("(p j) m -> p j m", j=PACK))
+            if g == 0:
+                for r in (2, 3):
+                    load_scales(nc.sync, r)
         nc.sync.dma_start(offsets[:], slot)
         nc.sync.dma_start(out=store[:], in_=mem)
         words = x_words.rearrange("z p c r -> p z (c r)")
@@ -46,9 +56,6 @@ def tile_picked_widxput_min_l_kernel(tc, x_words, x_scales, mem, w1, slot, out):
         for g in range(PASSES):
             nc.sync.dma_start(out=x_first[g][:].bitcast(I32), in_=words[:, g, :cut].bitcast(I32))
         nc.sync.dma_start(out=x_second[:].bitcast(I32), in_=words[:, :, cut:].bitcast(I32))
-        rows = x_scales.rearrange("z (q r) c -> r q z c", r=4)
-        for r in range(4):
-            nc.scalar.dma_start(out=x_plane[r:P:32, :, :].bitcast(I32), in_=rows[r].bitcast(I32))
 
         w_codes, w_plane = [], []
         grouped = []

@@ -46,9 +46,7 @@ def tile_picked_widxput_min_l_kernel(tc, x_words, x_scales, mem, w1, slot, out):
             load_scales(nc.scalar, r)
         for g in range(PASSES):
             nc.sync.dma_start(out=w_raw[g][:], in_=w1[g * P * PACK : (g + 1) * P * PACK, :].rearrange("(p j) m -> p j m", j=PACK))
-            if g == 0:
-                for r in (2, 3):
-                    load_scales(nc.sync, r)
+            load_scales(nc.sync, 2 + g)
         nc.sync.dma_start(offsets[:], slot)
         nc.sync.dma_start(out=store[:], in_=mem)
         words = x_words.rearrange("z p c r -> p z (c r)")

@@ -20,6 +20,7 @@ PASSES = K // (P * PACK)
 HALVES = ((0, 256), (256, 512))
 MINIMA = {0: ((0, 128), (128, 256)), 256: ((256, 512),)}
 SCATTER_AFTER = {0: (0, 128), 256: (128, 512)}
+X_LOADS = ((0, 0, 0, 128), (0, 0, 128, 256), (0, 1, 0, 256), (1, 0, 256, 384), (1, 0, 384, 512), (1, 1, 256, 384), (1, 1, 384, 512))
 GATHERS = ((0, 256), (256, 512))
 
 
@@ -33,9 +34,7 @@ def tile_picked_widxput_min_l_kernel(tc, x_words, x_scales, mem, w1, slot, out):
         store = keep.tile([P, U], F32, name="store")
         x_plane = keep.tile([P, PASSES, T], U8, name="x_plane", align_bytes=64)
         w_raw = [keep.tile([P, PACK, N], F32, name="w_raw%d" % g) for g in range(PASSES)]
-        x_first = [keep.tile([P, HALVES[0][1]], U32, name="x_first%d" % g, align_bytes=64) for g in range(PASSES)]
-        x_second = keep.tile([P, PASSES, T - HALVES[0][1]], U32, name="x_second", align_bytes=64)
-        x_codes = [[x_first[g][:] for g in range(PASSES)], [x_second[:, g, :] for g in range(PASSES)]]
+        x_codes = [[keep.tile([P, b - a], U32, name="x_codes%d_%d" % (a, g), align_bytes=64) for g in range(PASSES)] for a, b in HALVES]
 
         rows = x_scales.rearrange("z (q r) c -> r q z c", r=4)
 
@@ -50,10 +49,9 @@ def tile_picked_widxput_min_l_kernel(tc, x_words, x_scales, mem, w1, slot, out):
         nc.sync.dma_start(offsets[:], slot)
         nc.sync.dma_start(out=store[:], in_=mem)
         words = x_words.rearrange("z p c r -> p z (c r)")
-        cut = PACK * HALVES[0][1]
-        for g in range(PASSES):
-            nc.sync.dma_start(out=x_first[g][:].bitcast(I32), in_=words[:, g, :cut].bitcast(I32))
-        nc.sync.dma_start(out=x_second[:].bitcast(I32), in_=words[:, :, cut:].bitcast(I32))
+        for h, g, lo, hi in X_LOADS:
+            a = HALVES[h][0]
+            nc.sync.dma_start(out=x_codes[h][g][:, lo - a : hi - a].bitcast(I32), in_=words[:, g, PACK * lo : PACK * hi].bitcast(I32))
 
         w_codes, w_plane = [], []
         grouped = []

@@ -20,7 +20,6 @@ PASSES = K // (P * PACK)
 HALVES = ((0, 256), (256, 512))
 MINIMA = {0: ((0, 128), (128, 256)), 256: ((256, 512),)}
 SCATTER_AFTER = {0: (0, 128), 256: (128, 512)}
-X_LOADS = ((0, 0, 0, 128), (0, 0, 128, 256), (0, 1, 0, 256), (1, 0, 256, 384), (1, 0, 384, 512), (1, 1, 256, 384), (1, 1, 384, 512))
 GATHERS = ((0, 256), (256, 512))
 
 
@@ -32,26 +31,31 @@ def tile_picked_widxput_min_l_kernel(tc, x_words, x_scales, mem, w1, slot, out):
 
         offsets = keep.tile([P, T // 16], U16, name="offsets")
         store = keep.tile([P, U], F32, name="store")
-        x_plane = keep.tile([P, PASSES, T], U8, name="x_plane", align_bytes=64)
+        x_plane = [keep.tile([P, PASSES, b - a], U8, name="x_plane%d" % a, align_bytes=64) for a, b in HALVES]
         w_raw = [keep.tile([P, PACK, N], F32, name="w_raw%d" % g) for g in range(PASSES)]
-        x_codes = [[keep.tile([P, b - a], U32, name="x_codes%d_%d" % (a, g), align_bytes=64) for g in range(PASSES)] for a, b in HALVES]
+        x_first = [keep.tile([P, 256], U32, name="x_first%d" % g, align_bytes=64) for g in range(PASSES)]
+        x_second = keep.tile([P, PASSES, 256], U32, name="x_second", align_bytes=64)
+        x_codes = [[x_first[g][:] for g in range(PASSES)], [x_second[:, g, :] for g in range(PASSES)]]
 
         rows = x_scales.rearrange("z (q r) c -> r q z c", r=4)
 
-        def load_scales(queue, r):
-            queue.dma_start(out=x_plane[r:P:32, :, :].bitcast(I32), in_=rows[r].bitcast(I32))
+        def load_scales(queue, h, r):
+            a, b = HALVES[h]
+            queue.dma_start(out=x_plane[h][r:P:32, :, :].bitcast(I32), in_=rows[r][:, :, a:b].bitcast(I32))
 
         for r in (0, 1):
-            load_scales(nc.scalar, r)
+            load_scales(nc.scalar, 0, r)
         for g in range(PASSES):
             nc.sync.dma_start(out=w_raw[g][:], in_=w1[g * P * PACK : (g + 1) * P * PACK, :].rearrange("(p j) m -> p j m", j=PACK))
-            load_scales(nc.sync, 2 + g)
+            load_scales(nc.sync, 0, 2 + g)
         nc.sync.dma_start(offsets[:], slot)
         nc.sync.dma_start(out=store[:], in_=mem)
         words = x_words.rearrange("z p c r -> p z (c r)")
-        for h, g, lo, hi in X_LOADS:
-            a = HALVES[h][0]
-            nc.sync.dma_start(out=x_codes[h][g][:, lo - a : hi - a].bitcast(I32), in_=words[:, g, PACK * lo : PACK * hi].bitcast(I32))
+        for g in range(PASSES):
+            nc.sync.dma_start(out=x_first[g][:].bitcast(I32), in_=words[:, g, 0 : PACK * 256].bitcast(I32))
+        nc.sync.dma_start(out=x_second[:].bitcast(I32), in_=words[:, :, PACK * 256 : PACK * 512].bitcast(I32))
+        for r in range(4):
+            load_scales(nc.sync, 1, r)
 
         w_codes, w_plane = [], []
         grouped = []
@@ -80,7 +84,7 @@ def tile_picked_widxput_min_l_kernel(tc, x_words, x_scales, mem, w1, slot, out):
                         lhsT=w_codes[g][:].bitcast(FP8X4),
                         lhsT_scale=w_plane[g][:],
                         rhs=x_codes[h][g][:, ma - a : mb - a].bitcast(FP8X4),
-                        rhs_scale=x_plane[:, g, ma:mb],
+                        rhs_scale=x_plane[h][:, g, ma - a : mb - a],
                         start=(g == 0),
                         stop=(g == PASSES - 1),
                     )

@@ -32,7 +32,7 @@ def tile_picked_widxput_min_l_kernel(tc, x_words, x_scales, mem, w1, slot, out):
         offsets = keep.tile([P, T // 16], U16, name="offsets")
         store = keep.tile([P, U], F32, name="store")
         x_plane = [keep.tile([P, PASSES, b - a], U8, name="x_plane%d" % a, align_bytes=64) for a, b in HALVES]
-        w_raw = [keep.tile([P, PACK, N], F32, name="w_raw%d" % g) for g in range(PASSES)]
+        w_raw = keep.tile([P, PASSES, PACK, N], F32, name="w_raw")
         x_first = [keep.tile([P, 256], U32, name="x_first%d" % g, align_bytes=64) for g in range(PASSES)]
         x_second = keep.tile([P, PASSES, 256], U32, name="x_second", align_bytes=64)
         x_codes = [[x_first[g][:] for g in range(PASSES)], [x_second[:, g, :] for g in range(PASSES)]]
@@ -45,9 +45,9 @@ def tile_picked_widxput_min_l_kernel(tc, x_words, x_scales, mem, w1, slot, out):
 
         for r in (0, 1):
             load_scales(nc.scalar, 0, r)
-        for g in range(PASSES):
-            nc.sync.dma_start(out=w_raw[g][:], in_=w1[g * P * PACK : (g + 1) * P * PACK, :].rearrange("(p j) m -> p j m", j=PACK))
-            load_scales(nc.sync, 0, 2 + g)
+        nc.sync.dma_start(out=w_raw[:], in_=w1.rearrange("(g p j) m -> p g j m", g=PASSES, j=PACK))
+        for r in (2, 3):
+            load_scales(nc.sync, 0, r)
         nc.sync.dma_start(offsets[:], slot)
         nc.sync.dma_start(out=store[:], in_=mem)
         words = x_words.rearrange("z p c r -> p z (c r)")
@@ -61,7 +61,7 @@ def tile_picked_widxput_min_l_kernel(tc, x_words, x_scales, mem, w1, slot, out):
         grouped = []
         for g in range(PASSES):
             t = keep.tile([P, N, PACK], BF16, name="grouped%d" % g, align_bytes=64)
-            nc.vector.tensor_copy(out=t[:].rearrange("p (c i) j -> p c j i", i=4), in_=w_raw[g][:].rearrange("p j (c i) -> p c j i", i=4))
+            nc.vector.tensor_copy(out=t[:].rearrange("p (c i) j -> p c j i", i=4), in_=w_raw[:, g, :, :].rearrange("p j (c i) -> p c j i", i=4))
             grouped.append(t)
         for g in range(PASSES):
             c = keep.tile([P, N], U32, name="w_codes%d" % g, align_bytes=64)
@@ -92,4 +92,5 @@ def tile_picked_widxput_min_l_kernel(tc, x_words, x_scales, mem, w1, slot, out):
                 nc.vector.tensor_tensor(new[:, ma:mb], y[ma][:], old[:, ma:mb], MIN)
             sa, sb = SCATTER_AFTER[a]
             nc.vector.tensor_copy(store[:].indirect(offsets[:, sa // 16 : sb // 16]), new[:, sa:sb])
-        nc.sync.dma_start(out=out, in_=store[:])
+        for c in range(0, U, U // 2):
+            nc.sync.dma_start(out=out[:, c : c + U // 2], in_=store[:, c : c + U // 2])

@@ -18,7 +18,7 @@ P = 128
 PACK = 4
 PASSES = K // (P * PACK)
 HALVES = ((0, 256), (256, 512))
-MINIMA = {0: ((0, 128), (128, 256)), 256: ((256, 512),)}
+MINIMA = {0: ((0, 128), (128, 256)), 256: ((256, 384), (384, 512))}
 SCATTER_AFTER = {0: (0, 128), 256: (128, 512)}
 GATHERS = ((0, 256), (256, 512))
 
@@ -34,8 +34,10 @@ def tile_picked_widxput_min_l_kernel(tc, x_words, x_scales, mem, w1, slot, out):
         x_plane = [keep.tile([P, PASSES, b - a], U8, name="x_plane%d" % a, align_bytes=64) for a, b in HALVES]
         w_raw = keep.tile([P, PASSES, PACK, N], F32, name="w_raw")
         x_first = [keep.tile([P, 256], U32, name="x_first%d" % g, align_bytes=64) for g in range(PASSES)]
-        x_second = keep.tile([P, PASSES, 256], U32, name="x_second", align_bytes=64)
-        x_codes = [[x_first[g][:] for g in range(PASSES)], [x_second[:, g, :] for g in range(PASSES)]]
+        x_late = {c: keep.tile([P, PASSES, 128], U32, name="x_late%d" % c, align_bytes=64) for c in (256, 384)}
+
+        def x_codes(g, ma, mb):
+            return x_first[g][:, ma:mb] if ma < 256 else x_late[ma][:, g, :]
 
         rows = x_scales.rearrange("z (q r) c -> r q z c", r=4)
 
@@ -53,9 +55,10 @@ def tile_picked_widxput_min_l_kernel(tc, x_words, x_scales, mem, w1, slot, out):
         words = x_words.rearrange("z p c r -> p z (c r)")
         for g in range(PASSES):
             nc.sync.dma_start(out=x_first[g][:].bitcast(I32), in_=words[:, g, 0 : PACK * 256].bitcast(I32))
-        nc.sync.dma_start(out=x_second[:].bitcast(I32), in_=words[:, :, PACK * 256 : PACK * 512].bitcast(I32))
+        nc.sync.dma_start(out=x_late[256][:].bitcast(I32), in_=words[:, :, PACK * 256 : PACK * 384].bitcast(I32))
         for r in range(4):
             load_scales(nc.sync, 1, r)
+        nc.sync.dma_start(out=x_late[384][:].bitcast(I32), in_=words[:, :, PACK * 384 : PACK * 512].bitcast(I32))
 
         w_codes, w_plane = [], []
         grouped = []
@@ -77,20 +80,19 @@ def tile_picked_widxput_min_l_kernel(tc, x_words, x_scales, mem, w1, slot, out):
         new = keep.tile([P, T], F32, name="new")
         for h, (a, b) in enumerate(HALVES):
             y = {ma: psum.tile([P, mb - ma], F32, name="y%d" % ma) for ma, mb in MINIMA[a]}
-            for g in range(PASSES):
-                for ma, mb in MINIMA[a]:
-                    nc.tensor.matmul_mx(
-                        out=y[ma][:],
-                        lhsT=w_codes[g][:].bitcast(FP8X4),
-                        lhsT_scale=w_plane[g][:],
-                        rhs=x_codes[h][g][:, ma - a : mb - a].bitcast(FP8X4),
-                        rhs_scale=x_plane[h][:, g, ma - a : mb - a],
-                        start=(g == 0),
-                        stop=(g == PASSES - 1),
-                    )
+            order = [(g, m) for g in range(PASSES) for m in MINIMA[a]] if h == 0 else [(g, m) for m in MINIMA[a] for g in range(PASSES)]
+            for g, (ma, mb) in order:
+                nc.tensor.matmul_mx(
+                    out=y[ma][:],
+                    lhsT=w_codes[g][:].bitcast(FP8X4),
+                    lhsT_scale=w_plane[g][:],
+                    rhs=x_codes(g, ma, mb).bitcast(FP8X4),
+                    rhs_scale=x_plane[h][:, g, ma - a : mb - a],
+                    start=(g == 0),
+                    stop=(g == PASSES - 1),
+                )
             for ma, mb in MINIMA[a]:
                 nc.vector.tensor_tensor(new[:, ma:mb], y[ma][:], old[:, ma:mb], MIN)
             sa, sb = SCATTER_AFTER[a]
             nc.vector.tensor_copy(store[:].indirect(offsets[:, sa // 16 : sb // 16]), new[:, sa:sb])
-        for c in range(0, U, U // 2):
-            nc.sync.dma_start(out=out[:, c : c + U // 2], in_=store[:, c : c + U // 2])
+        nc.sync.dma_start(out=out, in_=store[:])

@@ -13,14 +13,18 @@ U16 = mybir.dt.uint16
 U8 = mybir.dt.uint8
 FP8X4 = mybir.dt.float8_e4m3fn_x4
 MIN = mybir.AluOpType.min
+COPY = mybir.ActivationFunctionType.Copy
 
 P = 128
 PACK = 4
 PASSES = K // (P * PACK)
-HALVES = ((0, 256), (256, 512))
-MINIMA = {0: ((0, 128), (128, 256)), 256: ((256, 384), (384, 512))}
-SCATTER_AFTER = {0: (0, 128), 256: (128, 512)}
-GATHERS = ((0, 256), (256, 512))
+GROUPS = ((0, 128), (128, 256), (256, 384), (384, 512))
+MINIMA = {a: ((a, b),) for a, b in GROUPS}
+SCALAR_GATHERS = ((0, 128), (128, 256))
+VECTOR_GATHERS = ((256, 384), (384, 512))
+SCALAR_SCATTERS = ((0, 128), (128, 352))
+VECTOR_SCATTER = (352, 512)
+STORES = ((0, 320), (320, 640), (640, 896), (896, 1024))
 
 
 def tile_picked_widxput_min_l_kernel(tc, x_words, x_scales, mem, w1, slot, out):
@@ -31,34 +35,36 @@ def tile_picked_widxput_min_l_kernel(tc, x_words, x_scales, mem, w1, slot, out):
 
         offsets = keep.tile([P, T // 16], U16, name="offsets")
         store = keep.tile([P, U], F32, name="store")
-        x_plane = [keep.tile([P, PASSES, b - a], U8, name="x_plane%d" % a, align_bytes=64) for a, b in HALVES]
+        x_plane = keep.tile([P, PASSES, T], U8, name="x_plane", align_bytes=64)
         w_raw = keep.tile([P, PASSES, PACK, N], F32, name="w_raw")
-        x_first = [keep.tile([P, 256], U32, name="x_first%d" % g, align_bytes=64) for g in range(PASSES)]
-        x_late = {c: keep.tile([P, PASSES, 128], U32, name="x_late%d" % c, align_bytes=64) for c in (256, 384)}
-
-        def x_codes(g, ma, mb):
-            return x_first[g][:, ma:mb] if ma < 256 else x_late[ma][:, g, :]
+        x_codes = {(a, g): keep.tile([P, b - a], U32, name="x_codes%d_%d" % (a, g), align_bytes=64)[:] for a, b in GROUPS[4:] for g in range(PASSES)}
+        x_both = {a: keep.tile([P, PASSES, b - a], U32, name="x_both%d" % a, align_bytes=64) for a, b in GROUPS[:4]}
+        for a in x_both:
+            for g in range(PASSES):
+                x_codes[a, g] = x_both[a][:, g, :]
 
         rows = x_scales.rearrange("z (q r) c -> r q z c", r=4)
 
-        def load_scales(queue, h, r):
-            a, b = HALVES[h]
-            queue.dma_start(out=x_plane[h][r:P:32, :, :].bitcast(I32), in_=rows[r][:, :, a:b].bitcast(I32))
+        def load_scales(queue, r):
+            queue.dma_start(out=x_plane[r:P:32, :, :].bitcast(I32), in_=rows[r].bitcast(I32))
 
         for r in (0, 1):
-            load_scales(nc.scalar, 0, r)
+            load_scales(nc.scalar, r)
         nc.sync.dma_start(out=w_raw[:], in_=w1.rearrange("(g p j) m -> p g j m", g=PASSES, j=PACK))
         for r in (2, 3):
-            load_scales(nc.sync, 0, r)
+            load_scales(nc.sync, r)
         nc.sync.dma_start(offsets[:], slot)
         nc.sync.dma_start(out=store[:], in_=mem)
         words = x_words.rearrange("z p c r -> p z (c r)")
-        for g in range(PASSES):
-            nc.sync.dma_start(out=x_first[g][:].bitcast(I32), in_=words[:, g, 0 : PACK * 256].bitcast(I32))
-        nc.sync.dma_start(out=x_late[256][:].bitcast(I32), in_=words[:, :, PACK * 256 : PACK * 384].bitcast(I32))
-        for r in range(4):
-            load_scales(nc.sync, 1, r)
-        nc.sync.dma_start(out=x_late[384][:].bitcast(I32), in_=words[:, :, PACK * 384 : PACK * 512].bitcast(I32))
+        for a, b in GROUPS[:4]:
+            nc.sync.dma_start(out=x_both[a][:].bitcast(I32), in_=words[:, :, PACK * a : PACK * b].bitcast(I32))
+        for a, b in GROUPS[4:]:
+            for g in range(PASSES):
+                nc.sync.dma_start(out=x_codes[a, g].bitcast(I32), in_=words[:, g, PACK * a : PACK * b].bitcast(I32))
+
+        warm = keep.tile([P, 2], F32, name="warm")
+        nc.gpsimd.memset(warm[:, 0:1], 0.0)
+        nc.scalar.activation(warm[:, 1:2], warm[:, 0:1], COPY)
 
         w_codes, w_plane = [], []
         grouped = []
@@ -73,26 +79,41 @@ def tile_picked_widxput_min_l_kernel(tc, x_words, x_scales, mem, w1, slot, out):
             w_codes.append(c)
             w_plane.append(s)
 
+        spare = keep.tile([P, U], F32, name="spare")
         old = keep.tile([P, T], F32, name="old")
-        for a, b in GATHERS:
-            nc.vector.tensor_copy(old[:, a:b], store[:].indirect(offsets[:, a // 16 : b // 16]))
-
         new = keep.tile([P, T], F32, name="new")
-        for h, (a, b) in enumerate(HALVES):
-            y = {ma: psum.tile([P, mb - ma], F32, name="y%d" % ma) for ma, mb in MINIMA[a]}
-            order = [(g, m) for g in range(PASSES) for m in MINIMA[a]] if h == 0 else [(g, m) for m in MINIMA[a] for g in range(PASSES)]
-            for g, (ma, mb) in order:
+        joined = keep.tile([P, U], F32, name="joined")
+
+        def entries(a, b):
+            return offsets[:, a // 16 : b // 16]
+
+        nc.vector.tensor_copy(spare[:], store[:])
+        for a, b in SCALAR_GATHERS:
+            nc.scalar.activation(old[:, a:b], store[:].indirect(entries(a, b)), COPY)
+
+        for a, b in GROUPS:
+            y = psum.tile([P, b - a], F32, name="y%d" % a)
+            for g in range(PASSES):
                 nc.tensor.matmul_mx(
-                    out=y[ma][:],
+                    out=y[:],
                     lhsT=w_codes[g][:].bitcast(FP8X4),
                     lhsT_scale=w_plane[g][:],
-                    rhs=x_codes(g, ma, mb).bitcast(FP8X4),
-                    rhs_scale=x_plane[h][:, g, ma - a : mb - a],
+                    rhs=x_codes[a, g].bitcast(FP8X4),
+                    rhs_scale=x_plane[:, g, a:b],
                     start=(g == 0),
                     stop=(g == PASSES - 1),
                 )
             for ma, mb in MINIMA[a]:
-                nc.vector.tensor_tensor(new[:, ma:mb], y[ma][:], old[:, ma:mb], MIN)
-            sa, sb = SCATTER_AFTER[a]
-            nc.vector.tensor_copy(store[:].indirect(offsets[:, sa // 16 : sb // 16]), new[:, sa:sb])
-        nc.sync.dma_start(out=out, in_=store[:])
+                nc.vector.tensor_tensor(new[:, ma:mb], y[:, ma - a : mb - a], old[:, ma:mb], MIN)
+            if a == 0:
+                for ga, gb in VECTOR_GATHERS:
+                    nc.vector.tensor_copy(old[:, ga:gb], store[:].indirect(entries(ga, gb)))
+
+        for window, (a, b) in zip((spare, store), SCALAR_SCATTERS):
+            nc.scalar.activation(window[:].indirect(entries(a, b)), new[:, a:b], COPY)
+        a, b = VECTOR_SCATTER
+        nc.vector.tensor_copy(spare[:].indirect(entries(a, b)), new[:, a:b])
+
+        for a, b in STORES:
+            nc.vector.tensor_tensor(joined[:, a:b], store[:, a:b], spare[:, a:b], MIN)
+            nc.sync.dma_start(out=out[:, a:b], in_=joined[:, a:b])

@@ -20,11 +20,11 @@ PACK = 4
 PASSES = K // (P * PACK)
 GROUPS = ((0, 128), (128, 256), (256, 384), (384, 512))
 MINIMA = {a: ((a, b),) for a, b in GROUPS}
-SCALAR_GATHERS = ((0, 128), (128, 256))
-VECTOR_GATHERS = ((256, 384), (384, 512))
+SCALAR_GATHERS = ((0, 128), (128, 384))
+VECTOR_GATHERS = ((384, 512),)
 SCALAR_SCATTERS = ((0, 128), (128, 352))
 VECTOR_SCATTER = (352, 512)
-STORES = ((0, 320), (320, 640), (640, 896), (896, 1024))
+STORES = ((0, 160), (160, 384), (384, 640), (640, 864), (864, 1024))
 
 
 def tile_picked_widxput_min_l_kernel(tc, x_words, x_scales, mem, w1, slot, out):
@@ -54,10 +54,11 @@ def tile_picked_widxput_min_l_kernel(tc, x_words, x_scales, mem, w1, slot, out):
         for r in (2, 3):
             load_scales(nc.sync, r)
         nc.sync.dma_start(offsets[:], slot)
-        nc.sync.dma_start(out=store[:], in_=mem)
         words = x_words.rearrange("z p c r -> p z (c r)")
         for a, b in GROUPS[:4]:
             nc.sync.dma_start(out=x_both[a][:].bitcast(I32), in_=words[:, :, PACK * a : PACK * b].bitcast(I32))
+            if a == 0:
+                nc.sync.dma_start(out=store[:], in_=mem)
         for a, b in GROUPS[4:]:
             for g in range(PASSES):
                 nc.sync.dma_start(out=x_codes[a, g].bitcast(I32), in_=words[:, g, PACK * a : PACK * b].bitcast(I32))

@@ -24,7 +24,7 @@ SCALAR_GATHERS = ((0, 128), (128, 384))
 VECTOR_GATHERS = ((384, 512),)
 SCALAR_SCATTERS = ((0, 128), (128, 352))
 VECTOR_SCATTER = (352, 512)
-STORES = ((0, 160), (160, 384), (384, 640), (640, 864), (864, 1024))
+STORES = ((0, 192), (192, 480), (480, 768), (768, 1024))
 
 
 def tile_picked_widxput_min_l_kernel(tc, x_words, x_scales, mem, w1, slot, out):
@@ -37,8 +37,8 @@ def tile_picked_widxput_min_l_kernel(tc, x_words, x_scales, mem, w1, slot, out):
         store = keep.tile([P, U], F32, name="store")
         x_plane = keep.tile([P, PASSES, T], U8, name="x_plane", align_bytes=64)
         w_raw = keep.tile([P, PASSES, PACK, N], F32, name="w_raw")
-        x_codes = {(a, g): keep.tile([P, b - a], U32, name="x_codes%d_%d" % (a, g), align_bytes=64)[:] for a, b in GROUPS[4:] for g in range(PASSES)}
-        x_both = {a: keep.tile([P, PASSES, b - a], U32, name="x_both%d" % a, align_bytes=64) for a, b in GROUPS[:4]}
+        x_codes = {(a, g): keep.tile([P, b - a], U32, name="x_codes%d_%d" % (a, g), align_bytes=64)[:] for a, b in GROUPS[3:] for g in range(PASSES)}
+        x_both = {a: keep.tile([P, PASSES, b - a], U32, name="x_both%d" % a, align_bytes=64) for a, b in GROUPS[:3]}
         for a in x_both:
             for g in range(PASSES):
                 x_codes[a, g] = x_both[a][:, g, :]
@@ -55,11 +55,11 @@ def tile_picked_widxput_min_l_kernel(tc, x_words, x_scales, mem, w1, slot, out):
             load_scales(nc.sync, r)
         nc.sync.dma_start(offsets[:], slot)
         words = x_words.rearrange("z p c r -> p z (c r)")
-        for a, b in GROUPS[:4]:
+        for a, b in GROUPS[:3]:
             nc.sync.dma_start(out=x_both[a][:].bitcast(I32), in_=words[:, :, PACK * a : PACK * b].bitcast(I32))
             if a == 0:
                 nc.sync.dma_start(out=store[:], in_=mem)
-        for a, b in GROUPS[4:]:
+        for a, b in GROUPS[3:]:
             for g in range(PASSES):
                 nc.sync.dma_start(out=x_codes[a, g].bitcast(I32), in_=words[:, g, PACK * a : PACK * b].bitcast(I32))
 

@@ -18,13 +18,10 @@ COPY = mybir.ActivationFunctionType.Copy
 P = 128
 PACK = 4
 PASSES = K // (P * PACK)
-GROUPS = ((0, 128), (128, 256), (256, 384), (384, 512))
-MINIMA = {a: ((a, b),) for a, b in GROUPS}
-SCALAR_GATHERS = ((0, 128), (128, 384))
-VECTOR_GATHERS = ((384, 512),)
-SCALAR_SCATTERS = ((0, 128), (128, 352))
-VECTOR_SCATTER = (352, 512)
-STORES = ((0, 192), (192, 480), (480, 768), (768, 1024))
+GROUPS = ((0, 128), (128, 256))
+LAST = (256, 512)
+SPLIT = 352
+STORES = ((0, 160), (160, 384), (384, 640), (640, 864), (864, 1024))
 
 
 def tile_picked_widxput_min_l_kernel(tc, x_words, x_scales, mem, w1, slot, out):
@@ -37,11 +34,10 @@ def tile_picked_widxput_min_l_kernel(tc, x_words, x_scales, mem, w1, slot, out):
         store = keep.tile([P, U], F32, name="store")
         x_plane = keep.tile([P, PASSES, T], U8, name="x_plane", align_bytes=64)
         w_raw = keep.tile([P, PASSES, PACK, N], F32, name="w_raw")
-        x_codes = {(a, g): keep.tile([P, b - a], U32, name="x_codes%d_%d" % (a, g), align_bytes=64)[:] for a, b in GROUPS[3:] for g in range(PASSES)}
-        x_both = {a: keep.tile([P, PASSES, b - a], U32, name="x_both%d" % a, align_bytes=64) for a, b in GROUPS[:3]}
-        for a in x_both:
-            for g in range(PASSES):
-                x_codes[a, g] = x_both[a][:, g, :]
+        x_both = {a: keep.tile([P, PASSES, b - a], U32, name="x_both%d" % a, align_bytes=64) for a, b in GROUPS}
+        x_codes = {(a, g): x_both[a][:, g, :] for a in x_both for g in range(PASSES)}
+        for g in range(PASSES):
+            x_codes[LAST[0], g] = keep.tile([P, LAST[1] - LAST[0]], U32, name="x_last%d" % g, align_bytes=64)[:]
 
         rows = x_scales.rearrange("z (q r) c -> r q z c", r=4)
 
@@ -55,24 +51,25 @@ def tile_picked_widxput_min_l_kernel(tc, x_words, x_scales, mem, w1, slot, out):
             load_scales(nc.sync, r)
         nc.sync.dma_start(offsets[:], slot)
         words = x_words.rearrange("z p c r -> p z (c r)")
-        for a, b in GROUPS[:3]:
+        for a, b in GROUPS:
             nc.sync.dma_start(out=x_both[a][:].bitcast(I32), in_=words[:, :, PACK * a : PACK * b].bitcast(I32))
             if a == 0:
                 nc.sync.dma_start(out=store[:], in_=mem)
-        for a, b in GROUPS[3:]:
-            for g in range(PASSES):
-                nc.sync.dma_start(out=x_codes[a, g].bitcast(I32), in_=words[:, g, PACK * a : PACK * b].bitcast(I32))
+        for g in range(PASSES):
+            nc.sync.dma_start(out=x_codes[LAST[0], g].bitcast(I32), in_=words[:, g, PACK * LAST[0] : PACK * LAST[1]].bitcast(I32))
 
         warm = keep.tile([P, 2], F32, name="warm")
         nc.gpsimd.memset(warm[:, 0:1], 0.0)
         nc.scalar.activation(warm[:, 1:2], warm[:, 0:1], COPY)
 
-        w_codes, w_plane = [], []
-        grouped = []
+        grouped = [keep.tile([P, N, PACK], BF16, name="grouped%d" % g, align_bytes=64) for g in range(PASSES)]
+
+        def rounding(g):
+            return grouped[g][:].rearrange("p (c i) j -> p c j i", i=4), w_raw[:, g, :, :].rearrange("p j (c i) -> p c j i", i=4)
+
         for g in range(PASSES):
-            t = keep.tile([P, N, PACK], BF16, name="grouped%d" % g, align_bytes=64)
-            nc.vector.tensor_copy(out=t[:].rearrange("p (c i) j -> p c j i", i=4), in_=w_raw[:, g, :, :].rearrange("p j (c i) -> p c j i", i=4))
-            grouped.append(t)
+            nc.vector.tensor_copy(*rounding(g))
+        w_codes, w_plane = [], []
         for g in range(PASSES):
             c = keep.tile([P, N], U32, name="w_codes%d" % g, align_bytes=64)
             s = keep.tile([P, N], U8, name="w_plane%d" % g, align_bytes=64)
@@ -89,10 +86,10 @@ def tile_picked_widxput_min_l_kernel(tc, x_words, x_scales, mem, w1, slot, out):
             return offsets[:, a // 16 : b // 16]
 
         nc.vector.tensor_copy(spare[:], store[:])
-        for a, b in SCALAR_GATHERS:
+        for a, b in ((0, 128), (128, 384)):
             nc.scalar.activation(old[:, a:b], store[:].indirect(entries(a, b)), COPY)
 
-        for a, b in GROUPS:
+        for a, b in GROUPS + (LAST,):
             y = psum.tile([P, b - a], F32, name="y%d" % a)
             for g in range(PASSES):
                 nc.tensor.matmul_mx(
@@ -104,16 +101,15 @@ def tile_picked_widxput_min_l_kernel(tc, x_words, x_scales, mem, w1, slot, out):
                     start=(g == 0),
                     stop=(g == PASSES - 1),
                 )
-            for ma, mb in MINIMA[a]:
+            cuts = (a, SPLIT, b) if a < SPLIT < b else (a, b)
+            for ma, mb in zip(cuts, cuts[1:]):
                 nc.vector.tensor_tensor(new[:, ma:mb], y[:, ma - a : mb - a], old[:, ma:mb], MIN)
             if a == 0:
-                for ga, gb in VECTOR_GATHERS:
-                    nc.vector.tensor_copy(old[:, ga:gb], store[:].indirect(entries(ga, gb)))
+                nc.vector.tensor_copy(old[:, 384:512], store[:].indirect(entries(384, 512)))
 
-        for window, (a, b) in zip((spare, store), SCALAR_SCATTERS):
-            nc.scalar.activation(window[:].indirect(entries(a, b)), new[:, a:b], COPY)
-        a, b = VECTOR_SCATTER
-        nc.vector.tensor_copy(spare[:].indirect(entries(a, b)), new[:, a:b])
+        nc.scalar.activation(spare[:].indirect(entries(0, 128)), new[:, 0:128], COPY)
+        nc.scalar.activation(spare[:].indirect(entries(SPLIT, T)), new[:, SPLIT:T], COPY)
+        nc.vector.tensor_copy(store[:].indirect(entries(128, SPLIT)), new[:, 128:SPLIT])
 
         for a, b in STORES:
             nc.vector.tensor_tensor(joined[:, a:b], store[:, a:b], spare[:, a:b], MIN)

@@ -21,7 +21,7 @@ PASSES = K // (P * PACK)
 GROUPS = ((0, 128), (128, 256))
 LAST = (256, 512)
 SPLIT = 352
-STORES = ((0, 160), (160, 384), (384, 640), (640, 864), (864, 1024))
+STORES = ((0, 128), (128, 320), (320, 512), (512, 768), (768, 1024))
 
 
 def tile_picked_widxput_min_l_kernel(tc, x_words, x_scales, mem, w1, slot, out):
@@ -30,14 +30,14 @@ def tile_picked_widxput_min_l_kernel(tc, x_words, x_scales, mem, w1, slot, out):
         keep = ctx.enter_context(tc.tile_pool(name="keep", bufs=1))
         psum = ctx.enter_context(tc.psum_pool(name="psum", bufs=1))
 
-        offsets = keep.tile([P, T // 16], U16, name="offsets")
-        store = keep.tile([P, U], F32, name="store")
-        x_plane = keep.tile([P, PASSES, T], U8, name="x_plane", align_bytes=64)
-        w_raw = keep.tile([P, PASSES, PACK, N], F32, name="w_raw")
-        x_both = {a: keep.tile([P, PASSES, b - a], U32, name="x_both%d" % a, align_bytes=64) for a, b in GROUPS}
+        offsets = keep.tile([P, T // 16], U16, name="offsets", align_bytes=256)
+        store = keep.tile([P, U], F32, name="store", align_bytes=256)
+        x_plane = keep.tile([P, PASSES, T], U8, name="x_plane", align_bytes=256)
+        w_raw = keep.tile([P, PASSES, PACK, N], F32, name="w_raw", align_bytes=256)
+        x_both = {a: keep.tile([P, PASSES, b - a], U32, name="x_both%d" % a, align_bytes=256) for a, b in GROUPS}
         x_codes = {(a, g): x_both[a][:, g, :] for a in x_both for g in range(PASSES)}
         for g in range(PASSES):
-            x_codes[LAST[0], g] = keep.tile([P, LAST[1] - LAST[0]], U32, name="x_last%d" % g, align_bytes=64)[:]
+            x_codes[LAST[0], g] = keep.tile([P, LAST[1] - LAST[0]], U32, name="x_last%d" % g, align_bytes=256)[:]
 
         rows = x_scales.rearrange("z (q r) c -> r q z c", r=4)
 
@@ -80,7 +80,7 @@ def tile_picked_widxput_min_l_kernel(tc, x_words, x_scales, mem, w1, slot, out):
         spare = keep.tile([P, U], F32, name="spare")
         old = keep.tile([P, T], F32, name="old")
         new = keep.tile([P, T], F32, name="new")
-        joined = keep.tile([P, U], F32, name="joined")
+        joined = keep.tile([P, U], F32, name="joined", align_bytes=256)
 
         def entries(a, b):
             return offsets[:, a // 16 : b // 16]

from contextlib import ExitStack

import concourse.mybir as mybir

K, T, N, U = 1024, 512, 128, 1024
FLOPS = 2 * K * T * N

F32 = mybir.dt.float32
BF16 = mybir.dt.bfloat16
I32 = mybir.dt.int32
U32 = mybir.dt.uint32
U16 = mybir.dt.uint16
U8 = mybir.dt.uint8
FP8X4 = mybir.dt.float8_e4m3fn_x4
MIN = mybir.AluOpType.min
COPY = mybir.ActivationFunctionType.Copy

P = 128
PACK = 4
PASSES = K // (P * PACK)
GROUPS = ((0, 128), (128, 256))
LAST = (256, 512)
SPLIT = 352
STORES = ((0, 128), (128, 320), (320, 512), (512, 768), (768, 1024))


def tile_picked_widxput_min_l_kernel(tc, x_words, x_scales, mem, w1, slot, out):
    nc = tc.nc
    with ExitStack() as ctx:
        keep = ctx.enter_context(tc.tile_pool(name="keep", bufs=1))
        psum = ctx.enter_context(tc.psum_pool(name="psum", bufs=1))

        offsets = keep.tile([P, T // 16], U16, name="offsets", align_bytes=256)
        store = keep.tile([P, U], F32, name="store", align_bytes=256)
        x_plane = keep.tile([P, PASSES, T], U8, name="x_plane", align_bytes=256)
        w_raw = keep.tile([P, PASSES, PACK, N], F32, name="w_raw", align_bytes=256)
        x_both = {a: keep.tile([P, PASSES, b - a], U32, name="x_both%d" % a, align_bytes=256) for a, b in GROUPS}
        x_codes = {(a, g): x_both[a][:, g, :] for a in x_both for g in range(PASSES)}
        for g in range(PASSES):
            x_codes[LAST[0], g] = keep.tile([P, LAST[1] - LAST[0]], U32, name="x_last%d" % g, align_bytes=256)[:]

        rows = x_scales.rearrange("z (q r) c -> r q z c", r=4)

        def load_scales(queue, r):
            queue.dma_start(out=x_plane[r:P:32, :, :].bitcast(I32), in_=rows[r].bitcast(I32))

        for r in (0, 1):
            load_scales(nc.scalar, r)
        nc.sync.dma_start(out=w_raw[:], in_=w1.rearrange("(g p j) m -> p g j m", g=PASSES, j=PACK))
        for r in (2, 3):
            load_scales(nc.sync, r)
        nc.sync.dma_start(offsets[:], slot)
        words = x_words.rearrange("z p c r -> p z (c r)")
        for a, b in GROUPS:
            nc.sync.dma_start(out=x_both[a][:].bitcast(I32), in_=words[:, :, PACK * a : PACK * b].bitcast(I32))
            if a == 0:
                nc.sync.dma_start(out=store[:], in_=mem)
        for g in range(PASSES):
            nc.sync.dma_start(out=x_codes[LAST[0], g].bitcast(I32), in_=words[:, g, PACK * LAST[0] : PACK * LAST[1]].bitcast(I32))

        warm = keep.tile([P, 2], F32, name="warm")
        nc.gpsimd.memset(warm[:, 0:1], 0.0)
        nc.scalar.activation(warm[:, 1:2], warm[:, 0:1], COPY)

        grouped = [keep.tile([P, N, PACK], BF16, name="grouped%d" % g, align_bytes=64) for g in range(PASSES)]

        def rounding(g):
            return grouped[g][:].rearrange("p (c i) j -> p c j i", i=4), w_raw[:, g, :, :].rearrange("p j (c i) -> p c j i", i=4)

        for g in range(PASSES):
            nc.vector.tensor_copy(*rounding(g))
        w_codes, w_plane = [], []
        for g in range(PASSES):
            c = keep.tile([P, N], U32, name="w_codes%d" % g, align_bytes=64)
            s = keep.tile([P, N], U8, name="w_plane%d" % g, align_bytes=64)
            nc.vector.quantize_mx(out=c[:].bitcast(FP8X4), scales=s[:], in_=grouped[g][:].rearrange("p m j -> p (m j)"))
            w_codes.append(c)
            w_plane.append(s)

        spare = keep.tile([P, U], F32, name="spare")
        old = keep.tile([P, T], F32, name="old")
        new = keep.tile([P, T], F32, name="new")
        joined = keep.tile([P, U], F32, name="joined", align_bytes=256)

        def entries(a, b):
            return offsets[:, a // 16 : b // 16]

        nc.vector.tensor_copy(spare[:], store[:])
        for a, b in ((0, 128), (128, 384)):
            nc.scalar.activation(old[:, a:b], store[:].indirect(entries(a, b)), COPY)

        for a, b in GROUPS + (LAST,):
            y = psum.tile([P, b - a], F32, name="y%d" % a)
            for g in range(PASSES):
                nc.tensor.matmul_mx(
                    out=y[:],
                    lhsT=w_codes[g][:].bitcast(FP8X4),
                    lhsT_scale=w_plane[g][:],
                    rhs=x_codes[a, g].bitcast(FP8X4),
                    rhs_scale=x_plane[:, g, a:b],
                    start=(g == 0),
                    stop=(g == PASSES - 1),
                )
            cuts = (a, SPLIT, b) if a < SPLIT < b else (a, b)
            for ma, mb in zip(cuts, cuts[1:]):
                nc.vector.tensor_tensor(new[:, ma:mb], y[:, ma - a : mb - a], old[:, ma:mb], MIN)
            if a == 0:
                nc.vector.tensor_copy(old[:, 384:512], store[:].indirect(entries(384, 512)))

        nc.scalar.activation(spare[:].indirect(entries(0, 128)), new[:, 0:128], COPY)
        nc.scalar.activation(spare[:].indirect(entries(SPLIT, T)), new[:, SPLIT:T], COPY)
        nc.vector.tensor_copy(store[:].indirect(entries(128, SPLIT)), new[:, 128:SPLIT])

        for a, b in STORES:
            nc.vector.tensor_tensor(joined[:, a:b], store[:, a:b], spare[:, a:b], MIN)
            nc.sync.dma_start(out=out[:, a:b], in_=joined[:, a:b])
